import numpy as np
import ml_dtypes


def mxq(x, axis, fmt="e4m3"):
    dtype, down = {"e4m3": (ml_dtypes.float8_e4m3fn, 7), "e5m2": (ml_dtypes.float8_e5m2, 14)}[fmt]
    v = np.moveaxis(np.asarray(x, np.float32).astype(ml_dtypes.bfloat16).astype(np.float64), axis, -1)
    blocks = v.reshape(v.shape[:-1] + (-1, 32))
    amax = np.abs(blocks).max(-1, keepdims=True)
    byte = np.maximum(np.where(amax > 0, np.frexp(amax)[1] - 1 + 127, 0) - down, 1)
    scale = np.exp2(byte - 127.0)
    codes = (blocks / scale).astype(np.float32).astype(dtype).astype(np.float64)
    return np.moveaxis((codes * scale).reshape(v.shape), -1, axis)


WIDE = False


def mx_kscale(k):
    if not WIDE:
        return np.ones(k)
    levels = np.array([10, -10, 5, -5, 0])
    if k % 512:
        return np.exp2(np.random.permutation(np.resize(levels, k // 32))).repeat(32)
    a = np.empty((k // 512, 16))
    for p in range(k // 512):
        a[p, :8] = np.random.permutation(np.resize(levels, 8))
        for g in range(8):
            far = levels[np.abs(levels - a[p, g]) >= 10]
            a[p, g + 8] = far[np.random.randint(len(far))]
    return np.exp2(a.ravel()).repeat(32)


def f64(x):
    return np.asarray(x).astype(np.float64)


def striped(idx):
    return np.tile(idx.reshape(-1, 16).T, (8, 1)).astype(np.uint16)


def unstriped(offs):
    return offs[:16].T.reshape(-1).astype(np.int64)


def striped8(idx):
    return np.concatenate([x.reshape(-1, 16).T for x in idx]).astype(np.uint16)


def runs(offs, k):
    lists = np.stack([offs[16 * r : 16 * r + 16].T.reshape(-1) for r in range(8)]).astype(np.int64)
    return lists[np.arange(k) % 512 // 64]


def pack_weight(w):
    k, n = w.shape
    w = f64(np.asarray(w, np.float32).astype(ml_dtypes.bfloat16)).reshape(k // 32, 32, n)
    amax = np.abs(w).max(1)
    byte = np.clip(np.where(amax > 0, np.frexp(amax)[1] - 1 + 127 - 7, 1), 1, 254)
    scaled = (w * np.exp2(127.0 - byte)[:, None, :]).reshape(k, n).astype(np.float32)
    words = np.ascontiguousarray(scaled.reshape(k // 512, 128, 4, n).transpose(0, 1, 3, 2)).astype(ml_dtypes.float8_e4m3fn).view(np.uint8)
    return words, np.ascontiguousarray(byte.astype(np.uint8).reshape(k // 512, 16, n))


def unpack_weight(words, scales):
    g, p, n, _ = words.shape
    vals = np.ascontiguousarray(words).view(ml_dtypes.float8_e4m3fn).astype(np.float64) * np.repeat(np.exp2(scales.astype(np.float64) - 127.0), 8, axis=1)[..., None]
    return vals.transpose(0, 1, 3, 2).reshape(g * 512, n)


def sigmoid(v):
    return 1.0 / (1.0 + np.exp(-np.maximum(v, -700.0)))

def planes(y):
    n, m = y.shape
    v = y.astype(np.float32).astype(ml_dtypes.bfloat16).astype(np.float64).reshape(n // 32, 32, m)
    top = np.abs(v).max(1)
    byte = np.clip(np.where(top > 0, np.frexp(top)[1] - 1 + 127 - 7, 1), 1, 254)
    codes = (v * np.exp2(127.0 - byte)[:, None, :]).reshape(n, m).astype(np.float32).astype(ml_dtypes.float8_e4m3fn).view(np.uint8)
    words = codes.reshape(n // 512, 128, 4, m).transpose(0, 1, 3, 2)
    return np.ascontiguousarray(words), np.ascontiguousarray(byte.astype(np.uint8).reshape(n // 512, 16, m))


K, T, S, N, H = 512, 2048, 512, 512, 512


def setup_inputs():
    n = np.random.standard_normal
    s = mx_kscale(K)[:, None]
    u = mx_kscale(S)
    packed_xT = pack_weight(n((K, T)) * s)
    return {
        "x_words": packed_xT[0],
        "x_scales": packed_xT[1],
        "wa": (n((K, H)) / np.sqrt(K) / s).astype(np.float32),
        "wb": (n((K, N)) / np.sqrt(K) / s).astype(np.float32),
        "sl": np.random.uniform(1.0, 2.0, (S, 1)).astype(np.float32),
        "th": (0.5 * n((S, 1))).astype(np.float32),
        "tau": np.random.uniform(0.3, 0.9, (S, 1)).astype(np.float32),
        "gt": (np.random.uniform(0.5, 1.5, (S, 1)) * u[:, None]).astype(np.float32),
        "gi": (np.random.uniform(0.5, 1.5, (S, 1)) / u[:, None]).astype(np.float32),
        "tau2": np.random.uniform(0.3, 0.9, (H, 1)).astype(np.float32),
        "offs": striped(np.random.permutation(T)[:S]),
        "two": striped(np.random.permutation(T)[:S]),
        "n1": striped8(np.stack([np.random.permutation(H) for _ in range(8)])),
        "n2": striped8(np.stack([np.random.permutation(N) for _ in range(8)])),
        "n3": striped8(np.stack([np.random.permutation(N) for _ in range(8)])),
        "n4": striped8(np.stack([np.random.permutation(N) for _ in range(8)])),
        "n5": striped8(np.stack([np.random.permutation(N) for _ in range(8)])),
    }


def reference(x_words, x_scales, wa, wb, sl, th, tau, gt, gi, tau2, offs, two, n1, n2, n3, n4, n5):
    xq = unpack_weight(x_words, x_scales)[:, unstriped(offs)]
    a = xq.T @ mxq(f64(wa), 0, "e4m3")
    sg = sigmoid(f64(sl) * (a[np.arange(S)[:, None], runs(n1, S)] - f64(th)))
    z = f64(gt) * (a * sg)
    x_two = unpack_weight(x_words, x_scales)[:, unstriped(two)]
    b = x_two.T @ mxq(f64(wb), 0, "e4m3")
    top = b.max(axis=1, keepdims=True)
    ea = np.exp(f64(tau) * (b[np.arange(S)[:, None], runs(n2, S)] - top))
    sm = b * ea
    ds = np.zeros((S, N))
    ds[np.arange(S)[:, None], runs(n3, S)] = sm
    z2 = f64(gi) * (2.0 * ds - (0.5 * b))
    cv = 0.0625 * ((mxq(z, 0, "e4m3").T @ mxq(z2, 0, "e4m3")))
    top2 = cv.max(axis=1, keepdims=True)
    ea2 = np.exp(f64(tau2) * (cv[np.arange(H)[:, None], runs(n4, H)] - top2))
    ea3 = np.exp(f64(tau2) * (cv[np.arange(H)[:, None], runs(n5, H)] - top2))
    out_0 = (ea2 * (cv[np.arange(H)[:, None], runs(n4, H)]) + ea3 * (cv[np.arange(H)[:, None], runs(n5, H)])) / (ea2 + ea3 + 0.125)
    return (out_0,) + planes(out_0)

@@ -1,0 +1,357 @@
+from contextlib import ExitStack
+
+import concourse.mybir as mybir
+
+K, T, S, N, H = 512, 2048, 512, 512, 512
+FLOPS = 2 * K * S * H + 2 * K * S * N + 2 * S * H * N
+
+F32 = mybir.dt.float32
+BF16 = mybir.dt.bfloat16
+I32 = mybir.dt.int32
+U32 = mybir.dt.uint32
+U16 = mybir.dt.uint16
+U8 = mybir.dt.uint8
+FP8X4 = mybir.dt.float8_e4m3fn_x4
+ACT = mybir.ActivationFunctionType
+ALU = mybir.AluOpType
+
+P = 128
+PACK = 4
+HALF = 256
+CHUNK = 128
+
+
+def entries(offsets, start, count):
+    return offsets[:, start // 16 : (start + count) // 16]
+
+
+def tile_picked_mombesaesdevo_none_po_kernel(
+    tc, x_words, x_scales, wa, wb, sl, th, tau, gt, gi, tau2, offs, two, n1, n2, n3, n4, n5, out_0, out_1, out_2
+):
+    nc = tc.nc
+    with ExitStack() as ctx:
+        sb = ctx.enter_context(tc.tile_pool(name="sb", bufs=1))
+        psum = ctx.enter_context(tc.psum_pool(name="psum", bufs=1))
+
+        def load_list(name, src):
+            tile = sb.tile([P, S // 16], U16, name=name)
+            nc.sync.dma_start(tile[:], src)
+            return tile
+
+        def load_rows(name, src):
+            tile = sb.tile([P, PACK], F32, name=name)
+            nc.sync.dma_start(out=tile[:], in_=src.rearrange("(p t) o -> p (t o)", t=PACK))
+            return tile
+
+        table_bytes = sb.tile([P, T], U8, name="table_bytes", align_bytes=64)
+        nc.gpsimd.memset(table_bytes[:].bitcast(I32), 0)
+        wb_rows = wb.rearrange("(p j) n -> p j n", j=PACK)
+        wb_raw = [sb.tile([P, PACK, HALF], F32, name=f"wb_raw{h}") for h in range(2)]
+        for q in range(4):
+            nc.sync.dma_start(
+                out=table_bytes[32 * q : 32 * q + 4, :].bitcast(I32),
+                in_=x_scales[0, 4 * q : 4 * q + 4, :].bitcast(I32),
+            )
+        two_t = load_list("two_t", two)
+        offs_t = load_list("offs_t", offs)
+        for h in range(2):
+            nc.sync.dma_start(out=wb_raw[h][:], in_=wb_rows[:, :, h * HALF : (h + 1) * HALF])
+        table_words = sb.tile([P, T], U32, name="table_words", align_bytes=64)
+        nc.sync.dma_start(
+            out=table_words[:].bitcast(I32), in_=x_words[0].rearrange("p n r -> p (n r)").bitcast(I32)
+        )
+        tau_t = load_rows("tau_t", tau)
+        n2_t = load_list("n2_t", n2)
+        sl_t = load_rows("sl_t", sl)
+        th_t = load_rows("th_t", th)
+        wa_raw = sb.tile([P, PACK, H], F32, name="wa_raw")
+        nc.sync.dma_start(out=wa_raw[:], in_=wa.rearrange("(p j) n -> p j n", j=PACK))
+        n3_t = load_list("n3_t", n3)
+        gi_t = load_rows("gi_t", gi)
+        n1_t = load_list("n1_t", n1)
+        gt_t = load_rows("gt_t", gt)
+        n4_t = load_list("n4_t", n4)
+        n5_t = load_list("n5_t", n5)
+        tau2_t = load_rows("tau2_t", tau2)
+
+        def pick(name, table, offsets, dtype):
+            picked = sb.tile([P, S], dtype, name=name, align_bytes=64)
+            nc.vector.tensor_copy(
+                out=picked[:].rearrange("p (t m) -> p m t", t=PACK), in_=table[:].indirect(offsets[:])
+            )
+            return picked
+
+        two_bytes = pick("two_bytes", table_bytes, two_t, U8)
+        offs_bytes = pick("offs_bytes", table_bytes, offs_t, U8)
+
+        def woven(tile):
+            return tile[:].rearrange("p (c i t) -> p c t i", i=4, t=PACK)
+
+        def planes(tile):
+            return tile[:].rearrange("p t (c i) -> p c t i", i=4)
+
+        wb_codes = sb.tile([P, N], U32, name="wb_codes", align_bytes=64)
+        wb_scales = sb.tile([P, N], U8, name="wb_scales", align_bytes=64)
+        wb_bf = [sb.tile([P, PACK * HALF], BF16, name=f"wb_bf{h}", align_bytes=64) for h in range(2)]
+        for h in range(2):
+            nc.scalar.activation(woven(wb_bf[h]), planes(wb_raw[h]), ACT.Copy)
+            cols = slice(h * HALF, (h + 1) * HALF)
+            nc.vector.quantize_mx(out=wb_codes[:, cols].bitcast(FP8X4), scales=wb_scales[:, cols], in_=wb_bf[h][:])
+
+        two_words = pick("two_words", table_words, two_t, U32)
+        offs_words = pick("offs_words", table_words, offs_t, U32)
+
+        def product(bank, words, scale_bytes, t, codes, scales):
+            cols = slice(t * P, (t + 1) * P)
+            nc.tensor.matmul_mx(
+                out=bank[:],
+                lhsT=words[:, cols].bitcast(FP8X4),
+                lhsT_scale=scale_bytes[:, cols],
+                rhs=codes[:].bitcast(FP8X4),
+                rhs_scale=scales[:],
+                start=True,
+                stop=True,
+            )
+
+        bias_a = sb.tile([P, PACK], F32, name="bias_a")
+        nc.vector.scalar_tensor_tensor(
+            out=bias_a[:], in0=sl_t[:], scalar=-1.0, in1=th_t[:], op0=ALU.mult, op1=ALU.mult
+        )
+        neg_tau = sb.tile([P, PACK], F32, name="neg_tau")
+        nc.scalar.activation(neg_tau[:], tau_t[:], ACT.Copy, scale=-1.0)
+
+        top = sb.tile([P, PACK], F32, name="top")
+        bias_b = sb.tile([P, PACK], F32, name="bias_b")
+        b_rows, ea = [], []
+
+        def weigh_b(dst, t, h):
+            col = slice(t, t + 1)
+            nc.scalar.activation(
+                dst,
+                b_rows[t][:].indirect(entries(n2_t, h * HALF, HALF)),
+                ACT.Exp,
+                bias=bias_b[:, col],
+                scale=tau_t[:, col],
+            )
+
+        for t in range(PACK):
+            col = slice(t, t + 1)
+            bank = psum.tile([P, N], F32, name=f"b_bank{t}", tag=f"first{t}")
+            product(bank, two_words, two_bytes, t, wb_codes, wb_scales)
+            rows = sb.tile([P, N], F32, name=f"b_rows{t}")
+            nc.vector.tensor_scalar(
+                out=rows[:], in0=bank[:], scalar1=1.0, scalar2=None, op0=ALU.mult, op1=ALU.max, accum_out=top[:, col]
+            )
+            nc.scalar.activation(bias_b[:, col], top[:, col], ACT.Copy, scale=neg_tau[:, col])
+            b_rows.append(rows)
+            last = t == PACK - 1
+            weights = sb.tile([P, HALF if last else N], F32, name=f"b_weights{t}", tag=f"b_weights{t}", align_bytes=64)
+            for h in range(1 if last else 2):
+                weigh_b(weights[:, h * HALF : (h + 1) * HALF], t, h)
+            ea.append(weights)
+
+        wa_bf = sb.tile([P, PACK * H], BF16, name="wa_bf", tag="after_wa", align_bytes=64)
+        nc.gpsimd.tensor_scalar(
+            out=wa_bf[:].rearrange("p (c t) -> p c t", t=PACK),
+            in0=wa_raw[:].rearrange("p t c -> p c t"),
+            scalar1=1.0,
+            scalar2=0.0,
+            op0=ALU.mult,
+            op1=ALU.add,
+        )
+
+        gi_twice = sb.tile([P, PACK], F32, name="gi_twice")
+        nc.scalar.activation(gi_twice[:], gi_t[:], ACT.Copy, scale=2.0)
+        gi_half = sb.tile([P, PACK], F32, name="gi_half")
+        nc.scalar.activation(gi_half[:], gi_t[:], ACT.Copy, scale=-0.5)
+        neg_tau2 = sb.tile([P, PACK], F32, name="neg_tau2", tag="neg_tau2", align_bytes=64)
+        nc.scalar.activation(neg_tau2[:], tau2_t[:], ACT.Copy, scale=-1.0)
+
+        wa_codes = sb.tile([P, H], U32, name="wa_codes", align_bytes=64)
+        wa_scales = sb.tile([P, H], U8, name="wa_scales", align_bytes=64)
+        nc.vector.quantize_mx(out=wa_codes[:].bitcast(FP8X4), scales=wa_scales[:], in_=wa_bf[:])
+
+        ds = []
+
+        def scatter(t, tag):
+            window = sb.tile([P, 2 * N], F32, name=f"ds{t}", tag=tag, align_bytes=64)
+            ds.append(window)
+            nc.vector.tensor_tensor(window[:].indirect(n3_t[:]), b_rows[t][:], ea[t][:], ALU.mult)
+
+        z2_bf = sb.tile([P, PACK, N], BF16, name="z2_bf")
+
+        def make_z2(t, tag):
+            col = slice(t, t + 1)
+            less = sb.tile([P, N], F32, name=f"less{t}", tag=tag)
+            nc.scalar.activation(less[:], b_rows[t][:], ACT.Copy, scale=gi_half[:, col])
+            nc.vector.scalar_tensor_tensor(
+                out=z2_bf[:, t, :], in0=ds[t][:, 0:N], scalar=gi_twice[:, col], in1=less[:], op0=ALU.mult, op1=ALU.add
+            )
+
+        z_bf = sb.tile([P, PACK, H], BF16, name="z_bf")
+
+        def make_z(t):
+            col = slice(t, t + 1)
+            bank = psum.tile([P, H], F32, name=f"a_bank{t}")
+            product(bank, offs_words, offs_bytes, t, wa_codes, wa_scales)
+            rows = sb.tile([P, H], F32, name=f"a_rows{t}", tag=f"a_rows{t}")
+            nc.scalar.copy(rows[:], bank[:])
+            sg = sb.tile([P, H], F32, name=f"sg{t}", tag=f"sg{t}", align_bytes=64)
+            for h in range(2):
+                nc.scalar.activation(
+                    sg[:, h * HALF : (h + 1) * HALF],
+                    rows[:].indirect(entries(n1_t, h * HALF, HALF)),
+                    ACT.Sigmoid,
+                    bias=bias_a[:, col],
+                    scale=sl_t[:, col],
+                )
+            nc.vector.scalar_tensor_tensor(
+                out=z_bf[:, t, :], in0=bank[:], scalar=gt_t[:, col], in1=sg[:], op0=ALU.mult, op1=ALU.mult
+            )
+
+        scatter(0, "after_wa")
+        scatter(1, "b_weights0")
+        make_z(0)
+        make_z2(0, "a_rows0")
+        scatter(2, "sg0")
+        for t in (1, 2):
+            make_z(t)
+            make_z2(t, f"a_rows{t}")
+        make_z(3)
+        late = sb.tile([P, HALF], F32, name="late_weights", tag="a_rows3")
+        weigh_b(late[:], 3, 1)
+        window = sb.tile([P, 2 * N], F32, name="ds3", tag="sg3", align_bytes=64)
+        ds.append(window)
+        for h, weights in enumerate((ea[3], late)):
+            nc.vector.tensor_tensor(
+                window[:].indirect(entries(n3_t, h * HALF, HALF)),
+                b_rows[3][:, h * HALF : (h + 1) * HALF],
+                weights[:],
+                ALU.mult,
+            )
+        make_z2(3, "less3")
+
+        z_woven = sb.tile([P, PACK * H], BF16, name="z_woven", align_bytes=64)
+        nc.scalar.copy(
+            z_woven[:].rearrange("p (u m t) -> p m t u", u=PACK, t=PACK),
+            z_bf[:].rearrange("p t (m u) -> p m t u", u=PACK),
+        )
+        z2_woven = sb.tile([P, PACK * N], BF16, name="z2_woven", align_bytes=64)
+        nc.vector.tensor_copy(out=woven(z2_woven), in_=planes(z2_bf))
+        z2_codes = sb.tile([P, N], U32, name="z2_codes", align_bytes=64)
+        z2_scales = sb.tile([P, N], U8, name="z2_scales", align_bytes=64)
+        nc.vector.quantize_mx(out=z2_codes[:].bitcast(FP8X4), scales=z2_scales[:], in_=z2_woven[:])
+        z_codes = sb.tile([P, H], U32, name="z_codes", align_bytes=64)
+        z_scales = sb.tile([P, H], U8, name="z_scales", align_bytes=64)
+        nc.vector.quantize_mx(out=z_codes[:].bitcast(FP8X4), scales=z_scales[:], in_=z_woven[:])
+
+        top2 = sb.tile([P, PACK], F32, name="top2", tag="top2", align_bytes=64)
+        bias_c = sb.tile([P, PACK], F32, name="bias_c")
+        cv = []
+        for t in range(PACK):
+            col = slice(t, t + 1)
+            bank = psum.tile([P, N], F32, name=f"cv_bank{t}", tag=f"first{t}")
+            product(bank, z_codes, z_scales, t, z2_codes, z2_scales)
+            rows = sb.tile([P, N], F32, name=f"cv{t}")
+            nc.vector.tensor_scalar(
+                out=rows[:], in0=bank[:], scalar1=0.0625, scalar2=None, op0=ALU.mult, op1=ALU.max, accum_out=top2[:, col]
+            )
+            nc.vector.tensor_tensor(bias_c[:, col], top2[:, col], neg_tau2[:, col], ALU.mult)
+            cv.append(rows)
+
+        def wide(name):
+            return sb.tile([P, PACK, N], F32, name=name, align_bytes=64)
+
+        lists = (n4_t, n5_t)
+        ea_first = sb.tile([P, 2, PACK, CHUNK], F32, name="ea_first", align_bytes=64)
+        ea_rest = sb.tile([P, 2, PACK, N - CHUNK], F32, name="ea_rest", tag="top2", align_bytes=64)
+        fetched = sb.tile([P, 2, PACK, N], F32, name="fetched", tag="neg_tau2", align_bytes=64)
+        den, root, inv = wide("den"), wide("root"), wide("inv")
+        prods = (wide("p2"), wide("p3"))
+        num, res = wide("num"), wide("res")
+
+        def weights_at(k, start, width):
+            if start < CHUNK:
+                return ea_first[:, k, :, start : start + width]
+            return ea_rest[:, k, :, start - CHUNK : start - CHUNK + width]
+
+        def weigh(t, start, width):
+            col = slice(t, t + 1)
+            for k in range(2):
+                nc.scalar.activation(
+                    weights_at(k, start, width)[:, t, :],
+                    cv[t][:].indirect(entries(lists[k], start, width)),
+                    ACT.Exp,
+                    bias=bias_c[:, col],
+                    scale=tau2_t[:, col],
+                )
+
+        def part(tile, c):
+            return tile[:, :, c * CHUNK : (c + 1) * CHUNK]
+
+        def total(c):
+            nc.vector.scalar_tensor_tensor(
+                out=part(den, c),
+                in0=weights_at(0, c * CHUNK, CHUNK),
+                scalar=0.125,
+                in1=weights_at(1, c * CHUNK, CHUNK),
+                op0=ALU.add,
+                op1=ALU.add,
+            )
+
+        for t in range(PACK):
+            weigh(t, 0, CHUNK)
+        total(0)
+        nc.vector.reciprocal(out=part(inv, 0), in_=part(den, 0))
+        for t in range(PACK):
+            weigh(t, CHUNK, 2 * CHUNK)
+        total(1)
+        total(2)
+        for t in range(PACK):
+            weigh(t, 3 * CHUNK, CHUNK)
+        total(3)
+
+        out_rows = out_0.rearrange("(p t) n -> p t n", t=PACK)
+        out_words = out_1[0].rearrange("p n r -> p (n r)").bitcast(I32)
+        codes = sb.tile([P, N], U32, name="out_codes", align_bytes=64)
+        scales = sb.tile([P, N], U8, name="out_scales", align_bytes=64)
+
+        def numerator(c):
+            cols = slice(c * CHUNK, (c + 1) * CHUNK)
+            for k in range(2):
+                for t in range(PACK):
+                    nc.scalar.activation(
+                        fetched[:, k, t, cols], cv[t][:].indirect(entries(lists[k], c * CHUNK, CHUNK)), ACT.Copy
+                    )
+                nc.vector.tensor_tensor(
+                    part(prods[k], c), weights_at(k, c * CHUNK, CHUNK), fetched[:, k, :, cols], ALU.mult
+                )
+            nc.vector.tensor_tensor(part(num, c), part(prods[0], c), part(prods[1], c), ALU.add)
+
+        def invert(c):
+            nc.scalar.activation(part(root, c), part(den, c), ACT.Abs_reciprocal_sqrt)
+            nc.vector.tensor_tensor(part(inv, c), part(root, c), part(root, c), ALU.mult)
+
+        def finish(c):
+            cols = slice(c * CHUNK, (c + 1) * CHUNK)
+            nc.vector.tensor_tensor(part(res, c), part(num, c), part(inv, c), ALU.mult)
+            nc.sync.dma_start(out=out_rows[:, :, cols], in_=part(res, c))
+            res_bf = sb.tile([P, PACK * CHUNK], BF16, name=f"res_bf{c}", align_bytes=64)
+            nc.vector.tensor_copy(out=woven(res_bf), in_=part(res, c).rearrange("p t (c i) -> p c t i", i=4))
+            nc.vector.quantize_mx(out=codes[:, cols].bitcast(FP8X4), scales=scales[:, cols], in_=res_bf[:])
+            nc.sync.dma_start(out=out_words[:, cols], in_=codes[:, cols].bitcast(I32))
+
+        numerator(0)
+        finish(0)
+        numerator(1)
+        invert(1)
+        finish(1)
+        invert(2)
+        invert(3)
+        for c in (2, 3):
+            numerator(c)
+            finish(c)
+        for q in range(4):
+            nc.scalar.dma_start(
+                out=out_2[0, 4 * q : 4 * q + 4, :].bitcast(I32), in_=scales[32 * q : 32 * q + 4, :].bitcast(I32)
+            )

@@ -54,25 +54,27 @@ def tile_picked_mombesaesdevo_none_po_kernel(
             )
         two_t = load_list("two_t", two)
         offs_t = load_list("offs_t", offs)
-        for h in range(2):
-            nc.sync.dma_start(out=wb_raw[h][:], in_=wb_rows[:, :, h * HALF : (h + 1) * HALF])
         table_words = sb.tile([P, T], U32, name="table_words", align_bytes=64)
         nc.sync.dma_start(
             out=table_words[:].bitcast(I32), in_=x_words[0].rearrange("p n r -> p (n r)").bitcast(I32)
         )
+        for h in range(2):
+            nc.sync.dma_start(out=wb_raw[h][:], in_=wb_rows[:, :, h * HALF : (h + 1) * HALF])
         tau_t = load_rows("tau_t", tau)
         n2_t = load_list("n2_t", n2)
         sl_t = load_rows("sl_t", sl)
         th_t = load_rows("th_t", th)
-        wa_raw = sb.tile([P, PACK, H], F32, name="wa_raw")
-        nc.sync.dma_start(out=wa_raw[:], in_=wa.rearrange("(p j) n -> p j n", j=PACK))
-        n3_t = load_list("n3_t", n3)
         gi_t = load_rows("gi_t", gi)
+        tau2_t = load_rows("tau2_t", tau2)
+        wa_rows = wa.rearrange("(p j) n -> p j n", j=PACK)
+        wa_raw = [sb.tile([P, PACK, HALF], F32, name=f"wa_raw{h}") for h in range(2)]
+        for h in range(2):
+            nc.sync.dma_start(out=wa_raw[h][:], in_=wa_rows[:, :, h * HALF : (h + 1) * HALF])
+        n3_t = load_list("n3_t", n3)
         n1_t = load_list("n1_t", n1)
         gt_t = load_rows("gt_t", gt)
         n4_t = load_list("n4_t", n4)
         n5_t = load_list("n5_t", n5)
-        tau2_t = load_rows("tau2_t", tau2)
 
         def pick(name, table, offsets, dtype):
             picked = sb.tile([P, S], dtype, name=name, align_bytes=64)
@@ -83,35 +85,37 @@ def tile_picked_mombesaesdevo_none_po_kernel(
 
         two_bytes = pick("two_bytes", table_bytes, two_t, U8)
         offs_bytes = pick("offs_bytes", table_bytes, offs_t, U8)
+        two_words = pick("two_words", table_words, two_t, U32)
+        offs_words = pick("offs_words", table_words, offs_t, U32)
 
         def woven(tile):
             return tile[:].rearrange("p (c i t) -> p c t i", i=4, t=PACK)
 
         def planes(tile):
-            return tile[:].rearrange("p t (c i) -> p c t i", i=4)
+            return tile.rearrange("p t (c i) -> p c t i", i=4)
 
         wb_codes = sb.tile([P, N], U32, name="wb_codes", align_bytes=64)
         wb_scales = sb.tile([P, N], U8, name="wb_scales", align_bytes=64)
         wb_bf = [sb.tile([P, PACK * HALF], BF16, name=f"wb_bf{h}", align_bytes=64) for h in range(2)]
         for h in range(2):
-            nc.scalar.activation(woven(wb_bf[h]), planes(wb_raw[h]), ACT.Copy)
+            nc.scalar.activation(woven(wb_bf[h]), planes(wb_raw[h][:]), ACT.Copy)
             cols = slice(h * HALF, (h + 1) * HALF)
             nc.vector.quantize_mx(out=wb_codes[:, cols].bitcast(FP8X4), scales=wb_scales[:, cols], in_=wb_bf[h][:])
 
-        two_words = pick("two_words", table_words, two_t, U32)
-        offs_words = pick("offs_words", table_words, offs_t, U32)
+        def product(bank, words, scale_bytes, t, codes, scales, spans):
+            rows = slice(t * P, (t + 1) * P)
+            for cols in spans:
+                nc.tensor.matmul_mx(
+                    out=bank[:, cols],
+                    lhsT=words[:, rows].bitcast(FP8X4),
+                    lhsT_scale=scale_bytes[:, rows],
+                    rhs=codes[:, cols].bitcast(FP8X4),
+                    rhs_scale=scales[:, cols],
+                    start=True,
+                    stop=True,
+                )
 
-        def product(bank, words, scale_bytes, t, codes, scales):
-            cols = slice(t * P, (t + 1) * P)
-            nc.tensor.matmul_mx(
-                out=bank[:],
-                lhsT=words[:, cols].bitcast(FP8X4),
-                lhsT_scale=scale_bytes[:, cols],
-                rhs=codes[:].bitcast(FP8X4),
-                rhs_scale=scales[:],
-                start=True,
-                stop=True,
-            )
+        left, right, whole = slice(0, HALF), slice(HALF, N), slice(0, N)
 
         bias_a = sb.tile([P, PACK], F32, name="bias_a")
         nc.vector.scalar_tensor_tensor(
@@ -120,8 +124,15 @@ def tile_picked_mombesaesdevo_none_po_kernel(
         neg_tau = sb.tile([P, PACK], F32, name="neg_tau")
         nc.scalar.activation(neg_tau[:], tau_t[:], ACT.Copy, scale=-1.0)
 
+        gi_twice = sb.tile([P, PACK], F32, name="gi_twice")
+        nc.scalar.activation(gi_twice[:], gi_t[:], ACT.Copy, scale=2.0)
+        gi_half = sb.tile([P, PACK], F32, name="gi_half", tag="gi_half", align_bytes=64)
+        nc.scalar.activation(gi_half[:], gi_t[:], ACT.Copy, scale=-0.5)
+        neg_tau2 = sb.tile([P, PACK], F32, name="neg_tau2", tag="neg_tau2", align_bytes=64)
+        nc.scalar.activation(neg_tau2[:], tau2_t[:], ACT.Copy, scale=-1.0)
+
         top = sb.tile([P, PACK], F32, name="top")
-        bias_b = sb.tile([P, PACK], F32, name="bias_b")
+        bias_b = sb.tile([P, PACK], F32, name="bias_b", tag="bias_b", align_bytes=64)
         b_rows, ea = [], []
 
         def weigh_b(dst, t, h):
@@ -137,7 +148,7 @@ def tile_picked_mombesaesdevo_none_po_kernel(
         for t in range(PACK):
             col = slice(t, t + 1)
             bank = psum.tile([P, N], F32, name=f"b_bank{t}", tag=f"first{t}")
-            product(bank, two_words, two_bytes, t, wb_codes, wb_scales)
+            product(bank, two_words, two_bytes, t, wb_codes, wb_scales, (left, right) if t == 0 else (whole,))
             rows = sb.tile([P, N], F32, name=f"b_rows{t}")
             nc.vector.tensor_scalar(
                 out=rows[:], in0=bank[:], scalar1=1.0, scalar2=None, op0=ALU.mult, op1=ALU.max, accum_out=top[:, col]
@@ -151,21 +162,15 @@ def tile_picked_mombesaesdevo_none_po_kernel(
             ea.append(weights)
 
         wa_bf = sb.tile([P, PACK * H], BF16, name="wa_bf", tag="after_wa", align_bytes=64)
-        nc.gpsimd.tensor_scalar(
-            out=wa_bf[:].rearrange("p (c t) -> p c t", t=PACK),
-            in0=wa_raw[:].rearrange("p t c -> p c t"),
-            scalar1=1.0,
-            scalar2=0.0,
-            op0=ALU.mult,
-            op1=ALU.add,
-        )
-
-        gi_twice = sb.tile([P, PACK], F32, name="gi_twice")
-        nc.scalar.activation(gi_twice[:], gi_t[:], ACT.Copy, scale=2.0)
-        gi_half = sb.tile([P, PACK], F32, name="gi_half")
-        nc.scalar.activation(gi_half[:], gi_t[:], ACT.Copy, scale=-0.5)
-        neg_tau2 = sb.tile([P, PACK], F32, name="neg_tau2", tag="neg_tau2", align_bytes=64)
-        nc.scalar.activation(neg_tau2[:], tau2_t[:], ACT.Copy, scale=-1.0)
+        for h in range(2):
+            nc.gpsimd.tensor_scalar(
+                out=wa_bf[:, h * PACK * HALF : (h + 1) * PACK * HALF].rearrange("p (c t) -> p c t", t=PACK),
+                in0=wa_raw[h][:].rearrange("p t c -> p c t"),
+                scalar1=1.0,
+                scalar2=0.0,
+                op0=ALU.mult,
+                op1=ALU.add,
+            )
 
         wa_codes = sb.tile([P, H], U32, name="wa_codes", align_bytes=64)
         wa_scales = sb.tile([P, H], U8, name="wa_scales", align_bytes=64)
@@ -180,43 +185,67 @@ def tile_picked_mombesaesdevo_none_po_kernel(
 
         z2_bf = sb.tile([P, PACK, N], BF16, name="z2_bf")
 
-        def make_z2(t, tag):
-            col = slice(t, t + 1)
-            less = sb.tile([P, N], F32, name=f"less{t}", tag=tag)
-            nc.scalar.activation(less[:], b_rows[t][:], ACT.Copy, scale=gi_half[:, col])
+        def scale_b(dst, t):
+            nc.scalar.activation(dst, b_rows[t][:], ACT.Copy, scale=gi_half[:, t : t + 1])
+
+        def make_z2(t, less, cols):
             nc.vector.scalar_tensor_tensor(
-                out=z2_bf[:, t, :], in0=ds[t][:, 0:N], scalar=gi_twice[:, col], in1=less[:], op0=ALU.mult, op1=ALU.add
+                out=z2_bf[:, t, cols],
+                in0=ds[t][:, cols],
+                scalar=gi_twice[:, t : t + 1],
+                in1=less[:, cols],
+                op0=ALU.mult,
+                op1=ALU.add,
             )
 
         z_bf = sb.tile([P, PACK, H], BF16, name="z_bf")
+        a_banks, a_rows = [], []
+
+        def make_a(t):
+            bank = psum.tile([P, H], F32, name=f"a_bank{t}")
+            product(bank, offs_words, offs_bytes, t, wa_codes, wa_scales, (whole,))
+            rows = sb.tile([P, H], F32, name=f"a_rows{t}", tag=f"a_rows{t}")
+            nc.scalar.copy(rows[:], bank[:])
+            a_banks.append(bank)
+            a_rows.append(rows)
 
         def make_z(t):
             col = slice(t, t + 1)
-            bank = psum.tile([P, H], F32, name=f"a_bank{t}")
-            product(bank, offs_words, offs_bytes, t, wa_codes, wa_scales)
-            rows = sb.tile([P, H], F32, name=f"a_rows{t}", tag=f"a_rows{t}")
-            nc.scalar.copy(rows[:], bank[:])
             sg = sb.tile([P, H], F32, name=f"sg{t}", tag=f"sg{t}", align_bytes=64)
             for h in range(2):
                 nc.scalar.activation(
                     sg[:, h * HALF : (h + 1) * HALF],
-                    rows[:].indirect(entries(n1_t, h * HALF, HALF)),
+                    a_rows[t][:].indirect(entries(n1_t, h * HALF, HALF)),
                     ACT.Sigmoid,
                     bias=bias_a[:, col],
                     scale=sl_t[:, col],
                 )
             nc.vector.scalar_tensor_tensor(
-                out=z_bf[:, t, :], in0=bank[:], scalar=gt_t[:, col], in1=sg[:], op0=ALU.mult, op1=ALU.mult
+                out=z_bf[:, t, :], in0=a_banks[t][:], scalar=gt_t[:, col], in1=sg[:], op0=ALU.mult, op1=ALU.mult
             )
 
         scatter(0, "after_wa")
         scatter(1, "b_weights0")
+        make_a(0)
+        make_a(1)
         make_z(0)
-        make_z2(0, "a_rows0")
+        less_first = sb.tile([P, N], F32, name="less_first", tag="a_rows0")
+        scale_b(less_first[:], 0)
+        make_z2(0, less_first, whole)
         scatter(2, "sg0")
+        make_a(2)
+        make_z(1)
+        make_a(3)
+        make_z(2)
+        less_mid = sb.tile([P, 2, N], F32, name="less_mid")
         for t in (1, 2):
-            make_z(t)
-            make_z2(t, f"a_rows{t}")
+            nc.vector.tensor_scalar(
+                out=less_mid[:, t - 1, :],
+                in0=b_rows[t][:],
+                scalar1=gi_half[:, t : t + 1],
+                scalar2=None,
+                op0=ALU.mult,
+            )
         make_z(3)
         late = sb.tile([P, HALF], F32, name="late_weights", tag="a_rows3")
         weigh_b(late[:], 3, 1)
@@ -229,21 +258,29 @@ def tile_picked_mombesaesdevo_none_po_kernel(
                 weights[:],
                 ALU.mult,
             )
-        make_z2(3, "less3")
+        less_last = sb.tile([P, N], F32, name="less_last", tag="bias_b", align_bytes=64)
+        scale_b(less_last[:], 3)
+        make_z2(1, less_mid[:, 0, :], whole)
+        make_z2(2, less_mid[:, 1, :], whole)
+        make_z2(3, less_last, left)
+        make_z2(3, less_last, right)
 
-        z_woven = sb.tile([P, PACK * H], BF16, name="z_woven", align_bytes=64)
+        z_woven = sb.tile([P, PACK * H], BF16, name="z_woven", tag="gi_half", align_bytes=64)
         nc.scalar.copy(
             z_woven[:].rearrange("p (u m t) -> p m t u", u=PACK, t=PACK),
             z_bf[:].rearrange("p t (m u) -> p m t u", u=PACK),
         )
-        z2_woven = sb.tile([P, PACK * N], BF16, name="z2_woven", align_bytes=64)
-        nc.vector.tensor_copy(out=woven(z2_woven), in_=planes(z2_bf))
+        z2_left = sb.tile([P, PACK * HALF], BF16, name="z2_left", align_bytes=64)
+        nc.scalar.copy(woven(z2_left), planes(z2_bf[:, :, left]))
+        z2_right = sb.tile([P, PACK * HALF], BF16, name="z2_right", align_bytes=64)
+        nc.vector.tensor_copy(out=woven(z2_right), in_=planes(z2_bf[:, :, right]))
         z2_codes = sb.tile([P, N], U32, name="z2_codes", align_bytes=64)
         z2_scales = sb.tile([P, N], U8, name="z2_scales", align_bytes=64)
-        nc.vector.quantize_mx(out=z2_codes[:].bitcast(FP8X4), scales=z2_scales[:], in_=z2_woven[:])
         z_codes = sb.tile([P, H], U32, name="z_codes", align_bytes=64)
         z_scales = sb.tile([P, H], U8, name="z_scales", align_bytes=64)
         nc.vector.quantize_mx(out=z_codes[:].bitcast(FP8X4), scales=z_scales[:], in_=z_woven[:])
+        nc.vector.quantize_mx(out=z2_codes[:, right].bitcast(FP8X4), scales=z2_scales[:, right], in_=z2_right[:])
+        nc.vector.quantize_mx(out=z2_codes[:, left].bitcast(FP8X4), scales=z2_scales[:, left], in_=z2_left[:])
 
         top2 = sb.tile([P, PACK], F32, name="top2", tag="top2", align_bytes=64)
         bias_c = sb.tile([P, PACK], F32, name="bias_c")
@@ -251,12 +288,12 @@ def tile_picked_mombesaesdevo_none_po_kernel(
         for t in range(PACK):
             col = slice(t, t + 1)
             bank = psum.tile([P, N], F32, name=f"cv_bank{t}", tag=f"first{t}")
-            product(bank, z_codes, z_scales, t, z2_codes, z2_scales)
+            product(bank, z_codes, z_scales, t, z2_codes, z2_scales, (right, left) if t == 0 else (whole,))
             rows = sb.tile([P, N], F32, name=f"cv{t}")
             nc.vector.tensor_scalar(
                 out=rows[:], in0=bank[:], scalar1=0.0625, scalar2=None, op0=ALU.mult, op1=ALU.max, accum_out=top2[:, col]
             )
-            nc.vector.tensor_tensor(bias_c[:, col], top2[:, col], neg_tau2[:, col], ALU.mult)
+            nc.scalar.activation(bias_c[:, col], top2[:, col], ACT.Copy, scale=neg_tau2[:, col])
             cv.append(rows)
 
         def wide(name):
@@ -264,9 +301,10 @@ def tile_picked_mombesaesdevo_none_po_kernel(
 
         lists = (n4_t, n5_t)
         ea_first = sb.tile([P, 2, PACK, CHUNK], F32, name="ea_first", align_bytes=64)
-        ea_rest = sb.tile([P, 2, PACK, N - CHUNK], F32, name="ea_rest", tag="top2", align_bytes=64)
-        fetched = sb.tile([P, 2, PACK, N], F32, name="fetched", tag="neg_tau2", align_bytes=64)
-        den, root, inv = wide("den"), wide("root"), wide("inv")
+        ea_rest = sb.tile([P, 2, PACK, N - CHUNK], F32, name="ea_rest", align_bytes=64)
+        fetched = [sb.tile([P, 2, PACK, HALF], F32, name="fetched_early", tag="neg_tau2", align_bytes=64)]
+        den = sb.tile([P, PACK, N], F32, name="den", tag="den", align_bytes=64)
+        root, inv = wide("root"), wide("inv")
         prods = (wide("p2"), wide("p3"))
         num, res = wide("num"), wide("res")
 
@@ -316,17 +354,25 @@ def tile_picked_mombesaesdevo_none_po_kernel(
         codes = sb.tile([P, N], U32, name="out_codes", align_bytes=64)
         scales = sb.tile([P, N], U8, name="out_scales", align_bytes=64)
 
+        pairs = (slice(0, 2), slice(2, 4))
+
         def numerator(c):
             cols = slice(c * CHUNK, (c + 1) * CHUNK)
+            values = fetched[c // 2][:, :, :, (c % 2) * CHUNK : (c % 2 + 1) * CHUNK]
             for k in range(2):
-                for t in range(PACK):
-                    nc.scalar.activation(
-                        fetched[:, k, t, cols], cv[t][:].indirect(entries(lists[k], c * CHUNK, CHUNK)), ACT.Copy
+                for pair in pairs:
+                    for t in range(pair.start, pair.stop):
+                        nc.scalar.activation(
+                            values[:, k, t, :], cv[t][:].indirect(entries(lists[k], c * CHUNK, CHUNK)), ACT.Copy
+                        )
+                    nc.vector.tensor_tensor(
+                        prods[k][:, pair, cols],
+                        weights_at(k, c * CHUNK, CHUNK)[:, pair, :],
+                        values[:, k, pair, :],
+                        ALU.mult,
                     )
-                nc.vector.tensor_tensor(
-                    part(prods[k], c), weights_at(k, c * CHUNK, CHUNK), fetched[:, k, :, cols], ALU.mult
-                )
-            nc.vector.tensor_tensor(part(num, c), part(prods[0], c), part(prods[1], c), ALU.add)
+            for pair in pairs:
+                nc.vector.tensor_tensor(num[:, pair, cols], prods[0][:, pair, cols], prods[1][:, pair, cols], ALU.add)
 
         def invert(c):
             nc.scalar.activation(part(root, c), part(den, c), ACT.Abs_reciprocal_sqrt)
@@ -334,10 +380,11 @@ def tile_picked_mombesaesdevo_none_po_kernel(
 
         def finish(c):
             cols = slice(c * CHUNK, (c + 1) * CHUNK)
-            nc.vector.tensor_tensor(part(res, c), part(num, c), part(inv, c), ALU.mult)
+            for pair in pairs:
+                nc.vector.tensor_tensor(res[:, pair, cols], num[:, pair, cols], inv[:, pair, cols], ALU.mult)
             nc.sync.dma_start(out=out_rows[:, :, cols], in_=part(res, c))
             res_bf = sb.tile([P, PACK * CHUNK], BF16, name=f"res_bf{c}", align_bytes=64)
-            nc.vector.tensor_copy(out=woven(res_bf), in_=part(res, c).rearrange("p t (c i) -> p c t i", i=4))
+            nc.vector.tensor_copy(out=woven(res_bf), in_=planes(part(res, c)))
             nc.vector.quantize_mx(out=codes[:, cols].bitcast(FP8X4), scales=scales[:, cols], in_=res_bf[:])
             nc.sync.dma_start(out=out_words[:, cols], in_=codes[:, cols].bitcast(I32))
 
@@ -348,6 +395,7 @@ def tile_picked_mombesaesdevo_none_po_kernel(
         finish(1)
         invert(2)
         invert(3)
+        fetched.append(sb.tile([P, 2, PACK, HALF], F32, name="fetched_late", tag="den", align_bytes=64))
         for c in (2, 3):
             numerator(c)
             finish(c)

@@ -67,7 +67,7 @@ def tile_picked_mombesaesdevo_none_po_kernel(
         gi_t = load_rows("gi_t", gi)
         tau2_t = load_rows("tau2_t", tau2)
         wa_rows = wa.rearrange("(p j) n -> p j n", j=PACK)
-        wa_raw = [sb.tile([P, PACK, HALF], F32, name=f"wa_raw{h}") for h in range(2)]
+        wa_raw = [sb.tile([P, PACK, HALF], F32, name=f"wa_raw{h}", tag=f"wa_raw{h}", align_bytes=64) for h in range(2)]
         for h in range(2):
             nc.sync.dma_start(out=wa_raw[h][:], in_=wa_rows[:, :, h * HALF : (h + 1) * HALF])
         n3_t = load_list("n3_t", n3)
@@ -96,7 +96,7 @@ def tile_picked_mombesaesdevo_none_po_kernel(
 
         wb_codes = sb.tile([P, N], U32, name="wb_codes", align_bytes=64)
         wb_scales = sb.tile([P, N], U8, name="wb_scales", align_bytes=64)
-        wb_bf = [sb.tile([P, PACK * HALF], BF16, name=f"wb_bf{h}", align_bytes=64) for h in range(2)]
+        wb_bf = [sb.tile([P, PACK * HALF], BF16, name=f"wb_bf{h}", tag=f"woven{h}", align_bytes=64) for h in range(2)]
         for h in range(2):
             nc.scalar.activation(woven(wb_bf[h]), planes(wb_raw[h][:]), ACT.Copy)
             cols = slice(h * HALF, (h + 1) * HALF)
@@ -126,13 +126,13 @@ def tile_picked_mombesaesdevo_none_po_kernel(
 
         gi_twice = sb.tile([P, PACK], F32, name="gi_twice")
         nc.scalar.activation(gi_twice[:], gi_t[:], ACT.Copy, scale=2.0)
-        gi_half = sb.tile([P, PACK], F32, name="gi_half", tag="gi_half", align_bytes=64)
+        gi_half = sb.tile([P, PACK], F32, name="gi_half")
         nc.scalar.activation(gi_half[:], gi_t[:], ACT.Copy, scale=-0.5)
         neg_tau2 = sb.tile([P, PACK], F32, name="neg_tau2", tag="neg_tau2", align_bytes=64)
         nc.scalar.activation(neg_tau2[:], tau2_t[:], ACT.Copy, scale=-1.0)
 
         top = sb.tile([P, PACK], F32, name="top")
-        bias_b = sb.tile([P, PACK], F32, name="bias_b", tag="bias_b", align_bytes=64)
+        bias_b = sb.tile([P, PACK], F32, name="bias_b")
         b_rows, ea = [], []
 
         def weigh_b(dst, t, h):
@@ -161,20 +161,20 @@ def tile_picked_mombesaesdevo_none_po_kernel(
                 weigh_b(weights[:, h * HALF : (h + 1) * HALF], t, h)
             ea.append(weights)
 
-        wa_bf = sb.tile([P, PACK * H], BF16, name="wa_bf", tag="after_wa", align_bytes=64)
+        wa_codes = sb.tile([P, H], U32, name="wa_codes", align_bytes=64)
+        wa_scales = sb.tile([P, H], U8, name="wa_scales", align_bytes=64)
         for h in range(2):
+            wa_bf = sb.tile([P, PACK * HALF], BF16, name=f"wa_bf{h}", tag=f"woven{1 - h}", align_bytes=64)
             nc.gpsimd.tensor_scalar(
-                out=wa_bf[:, h * PACK * HALF : (h + 1) * PACK * HALF].rearrange("p (c t) -> p c t", t=PACK),
+                out=wa_bf[:].rearrange("p (c t) -> p c t", t=PACK),
                 in0=wa_raw[h][:].rearrange("p t c -> p c t"),
                 scalar1=1.0,
                 scalar2=0.0,
                 op0=ALU.mult,
                 op1=ALU.add,
             )
-
-        wa_codes = sb.tile([P, H], U32, name="wa_codes", align_bytes=64)
-        wa_scales = sb.tile([P, H], U8, name="wa_scales", align_bytes=64)
-        nc.vector.quantize_mx(out=wa_codes[:].bitcast(FP8X4), scales=wa_scales[:], in_=wa_bf[:])
+            cols = slice(h * HALF, (h + 1) * HALF)
+            nc.vector.quantize_mx(out=wa_codes[:, cols].bitcast(FP8X4), scales=wa_scales[:, cols], in_=wa_bf[:])
 
         ds = []
 
@@ -183,10 +183,10 @@ def tile_picked_mombesaesdevo_none_po_kernel(
             ds.append(window)
             nc.vector.tensor_tensor(window[:].indirect(n3_t[:]), b_rows[t][:], ea[t][:], ALU.mult)
 
-        z2_bf = sb.tile([P, PACK, N], BF16, name="z2_bf")
-
         def scale_b(dst, t):
-            nc.scalar.activation(dst, b_rows[t][:], ACT.Copy, scale=gi_half[:, t : t + 1])
+            nc.gpsimd.tensor_scalar(
+                out=dst, in0=b_rows[t][:], scalar1=gi_half[:, t : t + 1], scalar2=0.0, op0=ALU.mult, op1=ALU.add
+            )
 
         def make_z2(t, less, cols):
             nc.vector.scalar_tensor_tensor(
@@ -204,14 +204,14 @@ def tile_picked_mombesaesdevo_none_po_kernel(
         def make_a(t):
             bank = psum.tile([P, H], F32, name=f"a_bank{t}")
             product(bank, offs_words, offs_bytes, t, wa_codes, wa_scales, (whole,))
-            rows = sb.tile([P, H], F32, name=f"a_rows{t}", tag=f"a_rows{t}")
+            rows = sb.tile([P, H], F32, name=f"a_rows{t}", tag=f"a_rows{t}", align_bytes=64)
             nc.scalar.copy(rows[:], bank[:])
             a_banks.append(bank)
             a_rows.append(rows)
 
         def make_z(t):
             col = slice(t, t + 1)
-            sg = sb.tile([P, H], F32, name=f"sg{t}", tag=f"sg{t}", align_bytes=64)
+            sg = sb.tile([P, H], F32, name=f"sg{t}")
             for h in range(2):
                 nc.scalar.activation(
                     sg[:, h * HALF : (h + 1) * HALF],
@@ -224,48 +224,47 @@ def tile_picked_mombesaesdevo_none_po_kernel(
                 out=z_bf[:, t, :], in0=a_banks[t][:], scalar=gt_t[:, col], in1=sg[:], op0=ALU.mult, op1=ALU.mult
             )
 
-        scatter(0, "after_wa")
-        scatter(1, "b_weights0")
+        scatter(0, "wa_raw1")
+        scatter(1, "woven0")
+        scatter(2, "b_weights0")
         make_a(0)
         make_a(1)
         make_z(0)
-        less_first = sb.tile([P, N], F32, name="less_first", tag="a_rows0")
-        scale_b(less_first[:], 0)
-        make_z2(0, less_first, whole)
-        scatter(2, "sg0")
+        less_pair = sb.tile([P, 2, N], F32, name="less_pair", tag="b_weights2", align_bytes=64)
+        for t in range(2):
+            scale_b(less_pair[:, t, :], t)
         make_a(2)
         make_z(1)
+        z2_bf = sb.tile([P, PACK, N], BF16, name="z2_bf", tag="a_rows1", align_bytes=64)
+        make_z2(0, less_pair[:, 0, :], whole)
+        less2 = sb.tile([P, N], F32, name="less2", tag="wa_raw1", align_bytes=64)
+        scale_b(less2[:], 2)
         make_a(3)
         make_z(2)
-        less_mid = sb.tile([P, 2, N], F32, name="less_mid")
-        for t in (1, 2):
-            nc.vector.tensor_scalar(
-                out=less_mid[:, t - 1, :],
-                in0=b_rows[t][:],
-                scalar1=gi_half[:, t : t + 1],
-                scalar2=None,
-                op0=ALU.mult,
-            )
-        make_z(3)
-        late = sb.tile([P, HALF], F32, name="late_weights", tag="a_rows3")
-        weigh_b(late[:], 3, 1)
-        window = sb.tile([P, 2 * N], F32, name="ds3", tag="sg3", align_bytes=64)
+        make_z2(1, less_pair[:, 1, :], whole)
+        window = sb.tile([P, 2 * N], F32, name="ds3", tag="a_rows2", align_bytes=64)
         ds.append(window)
-        for h, weights in enumerate((ea[3], late)):
+
+        def scatter_last(h, weights):
             nc.vector.tensor_tensor(
                 window[:].indirect(entries(n3_t, h * HALF, HALF)),
                 b_rows[3][:, h * HALF : (h + 1) * HALF],
                 weights[:],
                 ALU.mult,
             )
-        less_last = sb.tile([P, N], F32, name="less_last", tag="bias_b", align_bytes=64)
-        scale_b(less_last[:], 3)
-        make_z2(1, less_mid[:, 0, :], whole)
-        make_z2(2, less_mid[:, 1, :], whole)
-        make_z2(3, less_last, left)
-        make_z2(3, less_last, right)
 
-        z_woven = sb.tile([P, PACK * H], BF16, name="z_woven", tag="gi_half", align_bytes=64)
+        scatter_last(0, ea[3])
+        less3 = sb.tile([P, N], F32, name="less3", tag="b_weights3", align_bytes=64)
+        scale_b(less3[:], 3)
+        make_z(3)
+        late = sb.tile([P, HALF], F32, name="late_weights", tag="a_rows3", align_bytes=64)
+        weigh_b(late[:], 3, 1)
+        make_z2(2, less2, whole)
+        scatter_last(1, late)
+        make_z2(3, less3, left)
+        make_z2(3, less3, right)
+
+        z_woven = sb.tile([P, PACK * H], BF16, name="z_woven", align_bytes=64)
         nc.scalar.copy(
             z_woven[:].rearrange("p (u m t) -> p m t u", u=PACK, t=PACK),
             z_bf[:].rearrange("p t (m u) -> p m t u", u=PACK),
@@ -282,7 +281,7 @@ def tile_picked_mombesaesdevo_none_po_kernel(
         nc.vector.quantize_mx(out=z2_codes[:, right].bitcast(FP8X4), scales=z2_scales[:, right], in_=z2_right[:])
         nc.vector.quantize_mx(out=z2_codes[:, left].bitcast(FP8X4), scales=z2_scales[:, left], in_=z2_left[:])
 
-        top2 = sb.tile([P, PACK], F32, name="top2", tag="top2", align_bytes=64)
+        top2 = sb.tile([P, PACK], F32, name="top2")
         bias_c = sb.tile([P, PACK], F32, name="bias_c")
         cv = []
         for t in range(PACK):
@@ -303,7 +302,7 @@ def tile_picked_mombesaesdevo_none_po_kernel(
         ea_first = sb.tile([P, 2, PACK, CHUNK], F32, name="ea_first", align_bytes=64)
         ea_rest = sb.tile([P, 2, PACK, N - CHUNK], F32, name="ea_rest", align_bytes=64)
         fetched = [sb.tile([P, 2, PACK, HALF], F32, name="fetched_early", tag="neg_tau2", align_bytes=64)]
-        den = sb.tile([P, PACK, N], F32, name="den", tag="den", align_bytes=64)
+        den = [sb.tile([P, PACK, CHUNK], F32, name=f"den{c}", tag=f"den{c}", align_bytes=64) for c in range(4)]
         root, inv = wide("root"), wide("inv")
         prods = (wide("p2"), wide("p3"))
         num, res = wide("num"), wide("res")
@@ -329,7 +328,7 @@ def tile_picked_mombesaesdevo_none_po_kernel(
 
         def total(c):
             nc.vector.scalar_tensor_tensor(
-                out=part(den, c),
+                out=den[c][:],
                 in0=weights_at(0, c * CHUNK, CHUNK),
                 scalar=0.125,
                 in1=weights_at(1, c * CHUNK, CHUNK),
@@ -340,7 +339,7 @@ def tile_picked_mombesaesdevo_none_po_kernel(
         for t in range(PACK):
             weigh(t, 0, CHUNK)
         total(0)
-        nc.vector.reciprocal(out=part(inv, 0), in_=part(den, 0))
+        nc.vector.reciprocal(out=part(inv, 0), in_=den[0][:])
         for t in range(PACK):
             weigh(t, CHUNK, 2 * CHUNK)
         total(1)
@@ -375,7 +374,7 @@ def tile_picked_mombesaesdevo_none_po_kernel(
                 nc.vector.tensor_tensor(num[:, pair, cols], prods[0][:, pair, cols], prods[1][:, pair, cols], ALU.add)
 
         def invert(c):
-            nc.scalar.activation(part(root, c), part(den, c), ACT.Abs_reciprocal_sqrt)
+            nc.scalar.activation(part(root, c), den[c][:], ACT.Abs_reciprocal_sqrt)
             nc.vector.tensor_tensor(part(inv, c), part(root, c), part(root, c), ALU.mult)
 
         def finish(c):
@@ -395,7 +394,7 @@ def tile_picked_mombesaesdevo_none_po_kernel(
         finish(1)
         invert(2)
         invert(3)
-        fetched.append(sb.tile([P, 2, PACK, HALF], F32, name="fetched_late", tag="den", align_bytes=64))
+        fetched.append(sb.tile([P, 2, PACK, HALF], F32, name="fetched_late", tag="den2", align_bytes=64))
         for c in (2, 3):
             numerator(c)
             finish(c)

@@ -102,6 +102,9 @@ def tile_picked_mombesaesdevo_none_po_kernel(
             cols = slice(h * HALF, (h + 1) * HALF)
             nc.vector.quantize_mx(out=wb_codes[:, cols].bitcast(FP8X4), scales=wb_scales[:, cols], in_=wb_bf[h][:])
 
+        def quantise(codes, scales, cols, values):
+            nc.vector.quantize_mx(out=codes[:, cols].bitcast(FP8X4), scales=scales[:, cols], in_=values[:])
+
         def product(bank, words, scale_bytes, t, codes, scales, spans):
             rows = slice(t * P, (t + 1) * P)
             for cols in spans:
@@ -155,9 +158,8 @@ def tile_picked_mombesaesdevo_none_po_kernel(
             )
             nc.scalar.activation(bias_b[:, col], top[:, col], ACT.Copy, scale=neg_tau[:, col])
             b_rows.append(rows)
-            last = t == PACK - 1
-            weights = sb.tile([P, HALF if last else N], F32, name=f"b_weights{t}", tag=f"b_weights{t}", align_bytes=64)
-            for h in range(1 if last else 2):
+            weights = sb.tile([P, N], F32, name=f"b_weights{t}", tag=f"b_weights{t}", align_bytes=64)
+            for h in range(2):
                 weigh_b(weights[:, h * HALF : (h + 1) * HALF], t, h)
             ea.append(weights)
 
@@ -188,12 +190,12 @@ def tile_picked_mombesaesdevo_none_po_kernel(
                 out=dst, in0=b_rows[t][:], scalar1=gi_half[:, t : t + 1], scalar2=0.0, op0=ALU.mult, op1=ALU.add
             )
 
-        def make_z2(t, less, cols):
+        def make_z2(t, less):
             nc.vector.scalar_tensor_tensor(
-                out=z2_bf[:, t, cols],
-                in0=ds[t][:, cols],
+                out=z2_bf[:, t, :],
+                in0=ds[t][:, 0:N],
                 scalar=gi_twice[:, t : t + 1],
-                in1=less[:, cols],
+                in1=less,
                 op0=ALU.mult,
                 op1=ALU.add,
             )
@@ -224,180 +226,139 @@ def tile_picked_mombesaesdevo_none_po_kernel(
                 out=z_bf[:, t, :], in0=a_banks[t][:], scalar=gt_t[:, col], in1=sg[:], op0=ALU.mult, op1=ALU.mult
             )
 
-        scatter(0, "wa_raw1")
-        scatter(1, "woven0")
-        scatter(2, "b_weights0")
+        for t, tag in enumerate(("wa_raw1", "woven0", "b_weights0", "b_weights1")):
+            scatter(t, tag)
+        less_early = sb.tile([P, PACK - 1, N], F32, name="less_early", tag="b_weights3", align_bytes=64)
+        for t in range(PACK - 1):
+            scale_b(less_early[:, t, :], t)
         make_a(0)
-        make_a(1)
-        make_z(0)
-        less_pair = sb.tile([P, 2, N], F32, name="less_pair", tag="b_weights2", align_bytes=64)
-        for t in range(2):
-            scale_b(less_pair[:, t, :], t)
-        make_a(2)
-        make_z(1)
-        z2_bf = sb.tile([P, PACK, N], BF16, name="z2_bf", tag="a_rows1", align_bytes=64)
-        make_z2(0, less_pair[:, 0, :], whole)
-        less2 = sb.tile([P, N], F32, name="less2", tag="wa_raw1", align_bytes=64)
-        scale_b(less2[:], 2)
-        make_a(3)
-        make_z(2)
-        make_z2(1, less_pair[:, 1, :], whole)
-        window = sb.tile([P, 2 * N], F32, name="ds3", tag="a_rows2", align_bytes=64)
-        ds.append(window)
+        for t in range(PACK - 1):
+            make_a(t + 1)
+            make_z(t)
+        z2_bf = sb.tile([P, PACK, N], BF16, name="z2_bf", tag="a_rows2", align_bytes=64)
+        for t in range(PACK - 1):
+            make_z2(t, less_early[:, t, :])
+        less_last = sb.tile([P, N], F32, name="less_last", tag="b_weights0", align_bytes=64)
+        scale_b(less_last[:], PACK - 1)
+        make_z(PACK - 1)
+        make_z2(PACK - 1, less_last[:])
 
-        def scatter_last(h, weights):
-            nc.vector.tensor_tensor(
-                window[:].indirect(entries(n3_t, h * HALF, HALF)),
-                b_rows[3][:, h * HALF : (h + 1) * HALF],
-                weights[:],
-                ALU.mult,
-            )
-
-        scatter_last(0, ea[3])
-        less3 = sb.tile([P, N], F32, name="less3", tag="b_weights3", align_bytes=64)
-        scale_b(less3[:], 3)
-        make_z(3)
-        late = sb.tile([P, HALF], F32, name="late_weights", tag="a_rows3", align_bytes=64)
-        weigh_b(late[:], 3, 1)
-        make_z2(2, less2, whole)
-        scatter_last(1, late)
-        make_z2(3, less3, left)
-        make_z2(3, less3, right)
-
-        z_woven = sb.tile([P, PACK * H], BF16, name="z_woven", align_bytes=64)
-        nc.scalar.copy(
-            z_woven[:].rearrange("p (u m t) -> p m t u", u=PACK, t=PACK),
-            z_bf[:].rearrange("p t (m u) -> p m t u", u=PACK),
-        )
-        z2_left = sb.tile([P, PACK * HALF], BF16, name="z2_left", align_bytes=64)
-        nc.scalar.copy(woven(z2_left), planes(z2_bf[:, :, left]))
-        z2_right = sb.tile([P, PACK * HALF], BF16, name="z2_right", align_bytes=64)
-        nc.vector.tensor_copy(out=woven(z2_right), in_=planes(z2_bf[:, :, right]))
-        z2_codes = sb.tile([P, N], U32, name="z2_codes", align_bytes=64)
-        z2_scales = sb.tile([P, N], U8, name="z2_scales", align_bytes=64)
         z_codes = sb.tile([P, H], U32, name="z_codes", align_bytes=64)
         z_scales = sb.tile([P, H], U8, name="z_scales", align_bytes=64)
-        nc.vector.quantize_mx(out=z_codes[:].bitcast(FP8X4), scales=z_scales[:], in_=z_woven[:])
-        nc.vector.quantize_mx(out=z2_codes[:, right].bitcast(FP8X4), scales=z2_scales[:, right], in_=z2_right[:])
-        nc.vector.quantize_mx(out=z2_codes[:, left].bitcast(FP8X4), scales=z2_scales[:, left], in_=z2_left[:])
+        z2_codes = sb.tile([P, N], U32, name="z2_codes", align_bytes=64)
+        z2_scales = sb.tile([P, N], U8, name="z2_scales", align_bytes=64)
+        z_dealt = z_bf[:].rearrange("p t (m u) -> p m t u", u=PACK)
+        z_woven, z2_woven = [], []
+        for h in range(2):
+            tile = sb.tile([P, PACK * HALF], BF16, name=f"z_woven{h}", align_bytes=64)
+            nc.scalar.copy(tile[:].rearrange("p (u m t) -> p m t u", u=2, t=PACK), z_dealt[:, :, :, 2 * h : 2 * h + 2])
+            z_woven.append(tile)
+        for h, cols in enumerate((left, right)):
+            tile = sb.tile([P, PACK * HALF], BF16, name=f"z2_woven{h}", align_bytes=64)
+            nc.vector.tensor_copy(out=woven(tile), in_=planes(z2_bf[:, :, cols]))
+            z2_woven.append(tile)
+        quantise(z2_codes, z2_scales, left, z2_woven[0])
+        quantise(z_codes, z_scales, left, z_woven[0])
+        quantise(z2_codes, z2_scales, right, z2_woven[1])
+        quantise(z_codes, z_scales, right, z_woven[1])
 
         top2 = sb.tile([P, PACK], F32, name="top2")
-        bias_c = sb.tile([P, PACK], F32, name="bias_c")
-        cv = []
+        cv, bias_c = [], []
         for t in range(PACK):
             col = slice(t, t + 1)
             bank = psum.tile([P, N], F32, name=f"cv_bank{t}", tag=f"first{t}")
-            product(bank, z_codes, z_scales, t, z2_codes, z2_scales, (right, left) if t == 0 else (whole,))
+            product(bank, z_codes, z_scales, t, z2_codes, z2_scales, (left, right) if t == 0 else (whole,))
             rows = sb.tile([P, N], F32, name=f"cv{t}")
             nc.vector.tensor_scalar(
                 out=rows[:], in0=bank[:], scalar1=0.0625, scalar2=None, op0=ALU.mult, op1=ALU.max, accum_out=top2[:, col]
             )
-            nc.scalar.activation(bias_c[:, col], top2[:, col], ACT.Copy, scale=neg_tau2[:, col])
+            bias = sb.tile([P, 1], F32, name=f"bias_c{t}")
+            if t == 0:
+                nc.scalar.activation(bias[:], top2[:, col], ACT.Copy, scale=neg_tau2[:, col])
+            else:
+                nc.vector.tensor_tensor(bias[:], top2[:, col], neg_tau2[:, col], ALU.mult)
+            bias_c.append(bias)
             cv.append(rows)
 
         def wide(name):
             return sb.tile([P, PACK, N], F32, name=name, align_bytes=64)
 
         lists = (n4_t, n5_t)
-        ea_first = sb.tile([P, 2, PACK, CHUNK], F32, name="ea_first", align_bytes=64)
-        ea_rest = sb.tile([P, 2, PACK, N - CHUNK], F32, name="ea_rest", align_bytes=64)
-        fetched = [sb.tile([P, 2, PACK, HALF], F32, name="fetched_early", tag="neg_tau2", align_bytes=64)]
-        den = [sb.tile([P, PACK, CHUNK], F32, name=f"den{c}", tag=f"den{c}", align_bytes=64) for c in range(4)]
-        root, inv = wide("root"), wide("inv")
+        weights2 = (wide("ea_two"), wide("ea_three"))
         prods = (wide("p2"), wide("p3"))
-        num, res = wide("num"), wide("res")
+        inv, num, res = wide("inv"), wide("num"), wide("res")
 
-        def weights_at(k, start, width):
-            if start < CHUNK:
-                return ea_first[:, k, :, start : start + width]
-            return ea_rest[:, k, :, start - CHUNK : start - CHUNK + width]
-
-        def weigh(t, start, width):
-            col = slice(t, t + 1)
+        def weigh(t, cols):
             for k in range(2):
                 nc.scalar.activation(
-                    weights_at(k, start, width)[:, t, :],
-                    cv[t][:].indirect(entries(lists[k], start, width)),
+                    weights2[k][:, t, cols],
+                    cv[t][:].indirect(entries(lists[k], cols.start, cols.stop - cols.start)),
                     ACT.Exp,
-                    bias=bias_c[:, col],
-                    scale=tau2_t[:, col],
+                    bias=bias_c[t][:],
+                    scale=tau2_t[:, t : t + 1],
                 )
 
-        def part(tile, c):
-            return tile[:, :, c * CHUNK : (c + 1) * CHUNK]
-
-        def total(c):
+        def total(dst, tiles, cols):
             nc.vector.scalar_tensor_tensor(
-                out=den[c][:],
-                in0=weights_at(0, c * CHUNK, CHUNK),
+                out=dst,
+                in0=weights2[0][:, tiles, cols],
                 scalar=0.125,
-                in1=weights_at(1, c * CHUNK, CHUNK),
+                in1=weights2[1][:, tiles, cols],
                 op0=ALU.add,
                 op1=ALU.add,
             )
 
+        den_left = sb.tile([P, PACK, HALF], F32, name="den_left")
         for t in range(PACK):
-            weigh(t, 0, CHUNK)
-        total(0)
-        nc.vector.reciprocal(out=part(inv, 0), in_=den[0][:])
+            weigh(t, left)
         for t in range(PACK):
-            weigh(t, CHUNK, 2 * CHUNK)
-        total(1)
-        total(2)
+            total(den_left[:, t, :], t, left)
+            nc.vector.reciprocal(out=inv[:, t, left], in_=den_left[:, t, :])
         for t in range(PACK):
-            weigh(t, 3 * CHUNK, CHUNK)
-        total(3)
+            weigh(t, right)
+        quarters = (slice(HALF, HALF + CHUNK), slice(HALF + CHUNK, N))
+        den_right = []
+        for c, cols in enumerate(quarters):
+            den = sb.tile([P, PACK, CHUNK], F32, name=f"den_right{c}", tag=f"den_right{c}", align_bytes=64)
+            total(den[:], slice(0, PACK), cols)
+            den_right.append(den)
 
         out_rows = out_0.rearrange("(p t) n -> p t n", t=PACK)
         out_words = out_1[0].rearrange("p n r -> p (n r)").bitcast(I32)
         codes = sb.tile([P, N], U32, name="out_codes", align_bytes=64)
         scales = sb.tile([P, N], U8, name="out_scales", align_bytes=64)
-
         pairs = (slice(0, 2), slice(2, 4))
 
-        def numerator(c):
-            cols = slice(c * CHUNK, (c + 1) * CHUNK)
-            values = fetched[c // 2][:, :, :, (c % 2) * CHUNK : (c % 2 + 1) * CHUNK]
+        def finish(values, cols):
+            width = cols.stop - cols.start
             for k in range(2):
                 for pair in pairs:
                     for t in range(pair.start, pair.stop):
                         nc.scalar.activation(
-                            values[:, k, t, :], cv[t][:].indirect(entries(lists[k], c * CHUNK, CHUNK)), ACT.Copy
+                            values[:, k, t, :], cv[t][:].indirect(entries(lists[k], cols.start, width)), ACT.Copy
                         )
                     nc.vector.tensor_tensor(
-                        prods[k][:, pair, cols],
-                        weights_at(k, c * CHUNK, CHUNK)[:, pair, :],
-                        values[:, k, pair, :],
-                        ALU.mult,
+                        prods[k][:, pair, cols], weights2[k][:, pair, cols], values[:, k, pair, :], ALU.mult
                     )
             for pair in pairs:
                 nc.vector.tensor_tensor(num[:, pair, cols], prods[0][:, pair, cols], prods[1][:, pair, cols], ALU.add)
-
-        def invert(c):
-            nc.scalar.activation(part(root, c), den[c][:], ACT.Abs_reciprocal_sqrt)
-            nc.vector.tensor_tensor(part(inv, c), part(root, c), part(root, c), ALU.mult)
-
-        def finish(c):
-            cols = slice(c * CHUNK, (c + 1) * CHUNK)
             for pair in pairs:
                 nc.vector.tensor_tensor(res[:, pair, cols], num[:, pair, cols], inv[:, pair, cols], ALU.mult)
-            nc.sync.dma_start(out=out_rows[:, :, cols], in_=part(res, c))
-            res_bf = sb.tile([P, PACK * CHUNK], BF16, name=f"res_bf{c}", align_bytes=64)
-            nc.vector.tensor_copy(out=woven(res_bf), in_=planes(part(res, c)))
+            nc.sync.dma_start(out=out_rows[:, :, cols], in_=res[:, :, cols])
+            res_bf = sb.tile([P, PACK * width], BF16, name=f"res_bf{cols.start}", align_bytes=64)
+            nc.vector.tensor_copy(out=woven(res_bf), in_=planes(res[:, :, cols]))
             nc.vector.quantize_mx(out=codes[:, cols].bitcast(FP8X4), scales=scales[:, cols], in_=res_bf[:])
             nc.sync.dma_start(out=out_words[:, cols], in_=codes[:, cols].bitcast(I32))
 
-        numerator(0)
-        finish(0)
-        numerator(1)
-        invert(1)
-        finish(1)
-        invert(2)
-        invert(3)
-        fetched.append(sb.tile([P, 2, PACK, HALF], F32, name="fetched_late", tag="den2", align_bytes=64))
-        for c in (2, 3):
-            numerator(c)
-            finish(c)
+        values_left = sb.tile([P, 2, PACK, HALF], F32, name="values_left", tag="neg_tau2", align_bytes=64)
+        finish(values_left, left)
+        for c, cols in enumerate(quarters):
+            root = sb.tile([P, PACK, CHUNK], F32, name=f"root{c}")
+            nc.scalar.activation(root[:], den_right[c][:], ACT.Abs_reciprocal_sqrt)
+            nc.vector.tensor_tensor(inv[:, :, cols], root[:], root[:], ALU.mult)
+        values_right = sb.tile([P, 2, 2, PACK, CHUNK], F32, name="values_right", tag="den_right0", align_bytes=64)
+        for c, cols in enumerate(quarters):
+            finish(values_right[:, c], cols)
         for q in range(4):
             nc.scalar.dma_start(
                 out=out_2[0, 4 * q : 4 * q + 4, :].bitcast(I32), in_=scales[32 * q : 32 * q + 4, :].bitcast(I32)

@@ -243,6 +243,8 @@ def tile_picked_mombesaesdevo_none_po_kernel(
         make_z(PACK - 1)
         make_z2(PACK - 1, less_last[:])
 
+        warm = sb.tile([P, 1], F32, name="warm", tag="a_rows3", align_bytes=64)
+        nc.scalar.activation(warm[:], tau2_t[:, 0:1], ACT.Exp, scale=0.0)
         z_codes = sb.tile([P, H], U32, name="z_codes", align_bytes=64)
         z_scales = sb.tile([P, H], U8, name="z_scales", align_bytes=64)
         z2_codes = sb.tile([P, N], U32, name="z2_codes", align_bytes=64)

from contextlib import ExitStack

import concourse.mybir as mybir

K, T, S, N, H = 512, 2048, 512, 512, 512
FLOPS = 2 * K * S * H + 2 * K * S * N + 2 * S * H * N

F32 = mybir.dt.float32
BF16 = mybir.dt.bfloat16
I32 = mybir.dt.int32
U32 = mybir.dt.uint32
U16 = mybir.dt.uint16
U8 = mybir.dt.uint8
FP8X4 = mybir.dt.float8_e4m3fn_x4
ACT = mybir.ActivationFunctionType
ALU = mybir.AluOpType

P = 128
PACK = 4
HALF = 256
CHUNK = 128


def entries(offsets, start, count):
    return offsets[:, start // 16 : (start + count) // 16]


def tile_picked_mombesaesdevo_none_po_kernel(
    tc, x_words, x_scales, wa, wb, sl, th, tau, gt, gi, tau2, offs, two, n1, n2, n3, n4, n5, out_0, out_1, out_2
):
    nc = tc.nc
    with ExitStack() as ctx:
        sb = ctx.enter_context(tc.tile_pool(name="sb", bufs=1))
        psum = ctx.enter_context(tc.psum_pool(name="psum", bufs=1))

        def load_list(name, src):
            tile = sb.tile([P, S // 16], U16, name=name)
            nc.sync.dma_start(tile[:], src)
            return tile

        def load_rows(name, src):
            tile = sb.tile([P, PACK], F32, name=name)
            nc.sync.dma_start(out=tile[:], in_=src.rearrange("(p t) o -> p (t o)", t=PACK))
            return tile

        table_bytes = sb.tile([P, T], U8, name="table_bytes", align_bytes=64)
        nc.gpsimd.memset(table_bytes[:].bitcast(I32), 0)
        wb_rows = wb.rearrange("(p j) n -> p j n", j=PACK)
        wb_raw = [sb.tile([P, PACK, HALF], F32, name=f"wb_raw{h}") for h in range(2)]
        for q in range(4):
            nc.sync.dma_start(
                out=table_bytes[32 * q : 32 * q + 4, :].bitcast(I32),
                in_=x_scales[0, 4 * q : 4 * q + 4, :].bitcast(I32),
            )
        two_t = load_list("two_t", two)
        offs_t = load_list("offs_t", offs)
        table_words = sb.tile([P, T], U32, name="table_words", align_bytes=64)
        nc.sync.dma_start(
            out=table_words[:].bitcast(I32), in_=x_words[0].rearrange("p n r -> p (n r)").bitcast(I32)
        )
        for h in range(2):
            nc.sync.dma_start(out=wb_raw[h][:], in_=wb_rows[:, :, h * HALF : (h + 1) * HALF])
        tau_t = load_rows("tau_t", tau)
        n2_t = load_list("n2_t", n2)
        sl_t = load_rows("sl_t", sl)
        th_t = load_rows("th_t", th)
        gi_t = load_rows("gi_t", gi)
        tau2_t = load_rows("tau2_t", tau2)
        wa_rows = wa.rearrange("(p j) n -> p j n", j=PACK)
        wa_raw = [sb.tile([P, PACK, HALF], F32, name=f"wa_raw{h}", tag=f"wa_raw{h}", align_bytes=64) for h in range(2)]
        for h in range(2):
            nc.sync.dma_start(out=wa_raw[h][:], in_=wa_rows[:, :, h * HALF : (h + 1) * HALF])
        n3_t = load_list("n3_t", n3)
        n1_t = load_list("n1_t", n1)
        gt_t = load_rows("gt_t", gt)
        n4_t = load_list("n4_t", n4)
        n5_t = load_list("n5_t", n5)

        def pick(name, table, offsets, dtype):
            picked = sb.tile([P, S], dtype, name=name, align_bytes=64)
            nc.vector.tensor_copy(
                out=picked[:].rearrange("p (t m) -> p m t", t=PACK), in_=table[:].indirect(offsets[:])
            )
            return picked

        two_bytes = pick("two_bytes", table_bytes, two_t, U8)
        offs_bytes = pick("offs_bytes", table_bytes, offs_t, U8)
        two_words = pick("two_words", table_words, two_t, U32)
        offs_words = pick("offs_words", table_words, offs_t, U32)

        def woven(tile):
            return tile[:].rearrange("p (c i t) -> p c t i", i=4, t=PACK)

        def planes(tile):
            return tile.rearrange("p t (c i) -> p c t i", i=4)

        wb_codes = sb.tile([P, N], U32, name="wb_codes", align_bytes=64)
        wb_scales = sb.tile([P, N], U8, name="wb_scales", align_bytes=64)
        wb_bf = [sb.tile([P, PACK * HALF], BF16, name=f"wb_bf{h}", tag=f"woven{h}", align_bytes=64) for h in range(2)]
        for h in range(2):
            nc.scalar.activation(woven(wb_bf[h]), planes(wb_raw[h][:]), ACT.Copy)
            cols = slice(h * HALF, (h + 1) * HALF)
            nc.vector.quantize_mx(out=wb_codes[:, cols].bitcast(FP8X4), scales=wb_scales[:, cols], in_=wb_bf[h][:])

        def quantise(codes, scales, cols, values):
            nc.vector.quantize_mx(out=codes[:, cols].bitcast(FP8X4), scales=scales[:, cols], in_=values[:])

        def product(bank, words, scale_bytes, t, codes, scales, spans):
            rows = slice(t * P, (t + 1) * P)
            for cols in spans:
                nc.tensor.matmul_mx(
                    out=bank[:, cols],
                    lhsT=words[:, rows].bitcast(FP8X4),
                    lhsT_scale=scale_bytes[:, rows],
                    rhs=codes[:, cols].bitcast(FP8X4),
                    rhs_scale=scales[:, cols],
                    start=True,
                    stop=True,
                )

        left, right, whole = slice(0, HALF), slice(HALF, N), slice(0, N)

        bias_a = sb.tile([P, PACK], F32, name="bias_a")
        nc.vector.scalar_tensor_tensor(
            out=bias_a[:], in0=sl_t[:], scalar=-1.0, in1=th_t[:], op0=ALU.mult, op1=ALU.mult
        )
        neg_tau = sb.tile([P, PACK], F32, name="neg_tau")
        nc.scalar.activation(neg_tau[:], tau_t[:], ACT.Copy, scale=-1.0)

        gi_twice = sb.tile([P, PACK], F32, name="gi_twice")
        nc.scalar.activation(gi_twice[:], gi_t[:], ACT.Copy, scale=2.0)
        gi_half = sb.tile([P, PACK], F32, name="gi_half")
        nc.scalar.activation(gi_half[:], gi_t[:], ACT.Copy, scale=-0.5)
        neg_tau2 = sb.tile([P, PACK], F32, name="neg_tau2", tag="neg_tau2", align_bytes=64)
        nc.scalar.activation(neg_tau2[:], tau2_t[:], ACT.Copy, scale=-1.0)

        top = sb.tile([P, PACK], F32, name="top")
        bias_b = sb.tile([P, PACK], F32, name="bias_b")
        b_rows, ea = [], []

        def weigh_b(dst, t, h):
            col = slice(t, t + 1)
            nc.scalar.activation(
                dst,
                b_rows[t][:].indirect(entries(n2_t, h * HALF, HALF)),
                ACT.Exp,
                bias=bias_b[:, col],
                scale=tau_t[:, col],
            )

        for t in range(PACK):
            col = slice(t, t + 1)
            bank = psum.tile([P, N], F32, name=f"b_bank{t}", tag=f"first{t}")
            product(bank, two_words, two_bytes, t, wb_codes, wb_scales, (left, right) if t == 0 else (whole,))
            rows = sb.tile([P, N], F32, name=f"b_rows{t}")
            nc.vector.tensor_scalar(
                out=rows[:], in0=bank[:], scalar1=1.0, scalar2=None, op0=ALU.mult, op1=ALU.max, accum_out=top[:, col]
            )
            nc.scalar.activation(bias_b[:, col], top[:, col], ACT.Copy, scale=neg_tau[:, col])
            b_rows.append(rows)
            weights = sb.tile([P, N], F32, name=f"b_weights{t}", tag=f"b_weights{t}", align_bytes=64)
            for h in range(2):
                weigh_b(weights[:, h * HALF : (h + 1) * HALF], t, h)
            ea.append(weights)

        wa_codes = sb.tile([P, H], U32, name="wa_codes", align_bytes=64)
        wa_scales = sb.tile([P, H], U8, name="wa_scales", align_bytes=64)
        for h in range(2):
            wa_bf = sb.tile([P, PACK * HALF], BF16, name=f"wa_bf{h}", tag=f"woven{1 - h}", align_bytes=64)
            nc.gpsimd.tensor_scalar(
                out=wa_bf[:].rearrange("p (c t) -> p c t", t=PACK),
                in0=wa_raw[h][:].rearrange("p t c -> p c t"),
                scalar1=1.0,
                scalar2=0.0,
                op0=ALU.mult,
                op1=ALU.add,
            )
            cols = slice(h * HALF, (h + 1) * HALF)
            nc.vector.quantize_mx(out=wa_codes[:, cols].bitcast(FP8X4), scales=wa_scales[:, cols], in_=wa_bf[:])

        ds = []

        def scatter(t, tag):
            window = sb.tile([P, 2 * N], F32, name=f"ds{t}", tag=tag, align_bytes=64)
            ds.append(window)
            nc.vector.tensor_tensor(window[:].indirect(n3_t[:]), b_rows[t][:], ea[t][:], ALU.mult)

        def scale_b(dst, t):
            nc.gpsimd.tensor_scalar(
                out=dst, in0=b_rows[t][:], scalar1=gi_half[:, t : t + 1], scalar2=0.0, op0=ALU.mult, op1=ALU.add
            )

        def make_z2(t, less):
            nc.vector.scalar_tensor_tensor(
                out=z2_bf[:, t, :],
                in0=ds[t][:, 0:N],
                scalar=gi_twice[:, t : t + 1],
                in1=less,
                op0=ALU.mult,
                op1=ALU.add,
            )

        z_bf = sb.tile([P, PACK, H], BF16, name="z_bf")
        a_banks, a_rows = [], []

        def make_a(t):
            bank = psum.tile([P, H], F32, name=f"a_bank{t}")
            product(bank, offs_words, offs_bytes, t, wa_codes, wa_scales, (whole,))
            rows = sb.tile([P, H], F32, name=f"a_rows{t}", tag=f"a_rows{t}", align_bytes=64)
            nc.scalar.copy(rows[:], bank[:])
            a_banks.append(bank)
            a_rows.append(rows)

        def make_z(t):
            col = slice(t, t + 1)
            sg = sb.tile([P, H], F32, name=f"sg{t}")
            for h in range(2):
                nc.scalar.activation(
                    sg[:, h * HALF : (h + 1) * HALF],
                    a_rows[t][:].indirect(entries(n1_t, h * HALF, HALF)),
                    ACT.Sigmoid,
                    bias=bias_a[:, col],
                    scale=sl_t[:, col],
                )
            nc.vector.scalar_tensor_tensor(
                out=z_bf[:, t, :], in0=a_banks[t][:], scalar=gt_t[:, col], in1=sg[:], op0=ALU.mult, op1=ALU.mult
            )

        for t, tag in enumerate(("wa_raw1", "woven0", "b_weights0", "b_weights1")):
            scatter(t, tag)
        less_early = sb.tile([P, PACK - 1, N], F32, name="less_early", tag="b_weights3", align_bytes=64)
        for t in range(PACK - 1):
            scale_b(less_early[:, t, :], t)
        make_a(0)
        for t in range(PACK - 1):
            make_a(t + 1)
            make_z(t)
        z2_bf = sb.tile([P, PACK, N], BF16, name="z2_bf", tag="a_rows2", align_bytes=64)
        for t in range(PACK - 1):
            make_z2(t, less_early[:, t, :])
        less_last = sb.tile([P, N], F32, name="less_last", tag="b_weights0", align_bytes=64)
        scale_b(less_last[:], PACK - 1)
        make_z(PACK - 1)
        make_z2(PACK - 1, less_last[:])

        warm = sb.tile([P, 1], F32, name="warm", tag="a_rows3", align_bytes=64)
        nc.scalar.activation(warm[:], tau2_t[:, 0:1], ACT.Exp, scale=0.0)
        z_codes = sb.tile([P, H], U32, name="z_codes", align_bytes=64)
        z_scales = sb.tile([P, H], U8, name="z_scales", align_bytes=64)
        z2_codes = sb.tile([P, N], U32, name="z2_codes", align_bytes=64)
        z2_scales = sb.tile([P, N], U8, name="z2_scales", align_bytes=64)
        z_dealt = z_bf[:].rearrange("p t (m u) -> p m t u", u=PACK)
        z_woven, z2_woven = [], []
        for h in range(2):
            tile = sb.tile([P, PACK * HALF], BF16, name=f"z_woven{h}", align_bytes=64)
            nc.scalar.copy(tile[:].rearrange("p (u m t) -> p m t u", u=2, t=PACK), z_dealt[:, :, :, 2 * h : 2 * h + 2])
            z_woven.append(tile)
        for h, cols in enumerate((left, right)):
            tile = sb.tile([P, PACK * HALF], BF16, name=f"z2_woven{h}", align_bytes=64)
            nc.vector.tensor_copy(out=woven(tile), in_=planes(z2_bf[:, :, cols]))
            z2_woven.append(tile)
        quantise(z2_codes, z2_scales, left, z2_woven[0])
        quantise(z_codes, z_scales, left, z_woven[0])
        quantise(z2_codes, z2_scales, right, z2_woven[1])
        quantise(z_codes, z_scales, right, z_woven[1])

        top2 = sb.tile([P, PACK], F32, name="top2")
        cv, bias_c = [], []
        for t in range(PACK):
            col = slice(t, t + 1)
            bank = psum.tile([P, N], F32, name=f"cv_bank{t}", tag=f"first{t}")
            product(bank, z_codes, z_scales, t, z2_codes, z2_scales, (left, right) if t == 0 else (whole,))
            rows = sb.tile([P, N], F32, name=f"cv{t}")
            nc.vector.tensor_scalar(
                out=rows[:], in0=bank[:], scalar1=0.0625, scalar2=None, op0=ALU.mult, op1=ALU.max, accum_out=top2[:, col]
            )
            bias = sb.tile([P, 1], F32, name=f"bias_c{t}")
            if t == 0:
                nc.scalar.activation(bias[:], top2[:, col], ACT.Copy, scale=neg_tau2[:, col])
            else:
                nc.vector.tensor_tensor(bias[:], top2[:, col], neg_tau2[:, col], ALU.mult)
            bias_c.append(bias)
            cv.append(rows)

        def wide(name):
            return sb.tile([P, PACK, N], F32, name=name, align_bytes=64)

        lists = (n4_t, n5_t)
        weights2 = (wide("ea_two"), wide("ea_three"))
        prods = (wide("p2"), wide("p3"))
        inv, num, res = wide("inv"), wide("num"), wide("res")

        def weigh(t, cols):
            for k in range(2):
                nc.scalar.activation(
                    weights2[k][:, t, cols],
                    cv[t][:].indirect(entries(lists[k], cols.start, cols.stop - cols.start)),
                    ACT.Exp,
                    bias=bias_c[t][:],
                    scale=tau2_t[:, t : t + 1],
                )

        def total(dst, tiles, cols):
            nc.vector.scalar_tensor_tensor(
                out=dst,
                in0=weights2[0][:, tiles, cols],
                scalar=0.125,
                in1=weights2[1][:, tiles, cols],
                op0=ALU.add,
                op1=ALU.add,
            )

        den_left = sb.tile([P, PACK, HALF], F32, name="den_left")
        for t in range(PACK):
            weigh(t, left)
        for t in range(PACK):
            total(den_left[:, t, :], t, left)
            nc.vector.reciprocal(out=inv[:, t, left], in_=den_left[:, t, :])
        for t in range(PACK):
            weigh(t, right)
        quarters = (slice(HALF, HALF + CHUNK), slice(HALF + CHUNK, N))
        den_right = []
        for c, cols in enumerate(quarters):
            den = sb.tile([P, PACK, CHUNK], F32, name=f"den_right{c}", tag=f"den_right{c}", align_bytes=64)
            total(den[:], slice(0, PACK), cols)
            den_right.append(den)

        out_rows = out_0.rearrange("(p t) n -> p t n", t=PACK)
        out_words = out_1[0].rearrange("p n r -> p (n r)").bitcast(I32)
        codes = sb.tile([P, N], U32, name="out_codes", align_bytes=64)
        scales = sb.tile([P, N], U8, name="out_scales", align_bytes=64)
        pairs = (slice(0, 2), slice(2, 4))

        def finish(values, cols):
            width = cols.stop - cols.start
            for k in range(2):
                for pair in pairs:
                    for t in range(pair.start, pair.stop):
                        nc.scalar.activation(
                            values[:, k, t, :], cv[t][:].indirect(entries(lists[k], cols.start, width)), ACT.Copy
                        )
                    nc.vector.tensor_tensor(
                        prods[k][:, pair, cols], weights2[k][:, pair, cols], values[:, k, pair, :], ALU.mult
                    )
            for pair in pairs:
                nc.vector.tensor_tensor(num[:, pair, cols], prods[0][:, pair, cols], prods[1][:, pair, cols], ALU.add)
            for pair in pairs:
                nc.vector.tensor_tensor(res[:, pair, cols], num[:, pair, cols], inv[:, pair, cols], ALU.mult)
            nc.sync.dma_start(out=out_rows[:, :, cols], in_=res[:, :, cols])
            res_bf = sb.tile([P, PACK * width], BF16, name=f"res_bf{cols.start}", align_bytes=64)
            nc.vector.tensor_copy(out=woven(res_bf), in_=planes(res[:, :, cols]))
            nc.vector.quantize_mx(out=codes[:, cols].bitcast(FP8X4), scales=scales[:, cols], in_=res_bf[:])
            nc.sync.dma_start(out=out_words[:, cols], in_=codes[:, cols].bitcast(I32))

        values_left = sb.tile([P, 2, PACK, HALF], F32, name="values_left", tag="neg_tau2", align_bytes=64)
        finish(values_left, left)
        for c, cols in enumerate(quarters):
            root = sb.tile([P, PACK, CHUNK], F32, name=f"root{c}")
            nc.scalar.activation(root[:], den_right[c][:], ACT.Abs_reciprocal_sqrt)
            nc.vector.tensor_tensor(inv[:, :, cols], root[:], root[:], ALU.mult)
        values_right = sb.tile([P, 2, 2, PACK, CHUNK], F32, name="values_right", tag="den_right0", align_bytes=64)
        for c, cols in enumerate(quarters):
            finish(values_right[:, c], cols)
        for q in range(4):
            nc.scalar.dma_start(
                out=out_2[0, 4 * q : 4 * q + 4, :].bitcast(I32), in_=scales[32 * q : 32 * q + 4, :].bitcast(I32)
            )
